import numpy as np
import ml_dtypes


def mxq(x, axis, fmt="e4m3"):
    dtype, down = {"e4m3": (ml_dtypes.float8_e4m3fn, 7), "e5m2": (ml_dtypes.float8_e5m2, 14)}[fmt]
    v = np.moveaxis(np.asarray(x, np.float32).astype(ml_dtypes.bfloat16).astype(np.float64), axis, -1)
    blocks = v.reshape(v.shape[:-1] + (-1, 32))
    amax = np.abs(blocks).max(-1, keepdims=True)
    byte = np.maximum(np.where(amax > 0, np.frexp(amax)[1] - 1 + 127, 0) - down, 1)
    scale = np.exp2(byte - 127.0)
    codes = (blocks / scale).astype(np.float32).astype(dtype).astype(np.float64)
    return np.moveaxis((codes * scale).reshape(v.shape), -1, axis)


WIDE = False


def mx_kscale(k):
    if not WIDE:
        return np.ones(k)
    levels = np.array([10, -10, 5, -5, 0])
    if k % 512:
        return np.exp2(np.random.permutation(np.resize(levels, k // 32))).repeat(32)
    a = np.empty((k // 512, 16))
    for p in range(k // 512):
        a[p, :8] = np.random.permutation(np.resize(levels, 8))
        for g in range(8):
            far = levels[np.abs(levels - a[p, g]) >= 10]
            a[p, g + 8] = far[np.random.randint(len(far))]
    return np.exp2(a.ravel()).repeat(32)


def f64(x):
    return np.asarray(x).astype(np.float64)


def striped(idx):
    return np.tile(idx.reshape(-1, 16).T, (8, 1)).astype(np.uint16)


def unstriped(offs):
    return offs[:16].T.reshape(-1).astype(np.int64)


def striped8(idx):
    return np.concatenate([x.reshape(-1, 16).T for x in idx]).astype(np.uint16)


def runs(offs, k):
    lists = np.stack([offs[16 * r : 16 * r + 16].T.reshape(-1) for r in range(8)]).astype(np.int64)
    return lists[np.arange(k) % 512 // 64]


def pack_weight(w):
    k, n = w.shape
    w = f64(np.asarray(w, np.float32).astype(ml_dtypes.bfloat16)).reshape(k // 32, 32, n)
    amax = np.abs(w).max(1)
    byte = np.clip(np.where(amax > 0, np.frexp(amax)[1] - 1 + 127 - 7, 1), 1, 254)
    scaled = (w * np.exp2(127.0 - byte)[:, None, :]).reshape(k, n).astype(np.float32)
    words = np.ascontiguousarray(scaled.reshape(k // 512, 128, 4, n).transpose(0, 1, 3, 2)).astype(ml_dtypes.float8_e4m3fn).view(np.uint8)
    return words, np.ascontiguousarray(byte.astype(np.uint8).reshape(k // 512, 16, n))


def unpack_weight(words, scales):
    g, p, n, _ = words.shape
    vals = np.ascontiguousarray(words).view(ml_dtypes.float8_e4m3fn).astype(np.float64) * np.repeat(np.exp2(scales.astype(np.float64) - 127.0), 8, axis=1)[..., None]
    return vals.transpose(0, 1, 3, 2).reshape(g * 512, n)


K, T, S, N, G, H = 512, 2048, 512, 512, 2048, 512


def setup_inputs():
    n = np.random.standard_normal
    s = mx_kscale(K)[:, None]
    u = mx_kscale(S)
    packed_xT = pack_weight(n((K, T)) * s)
    packed_dT = pack_weight(n((K, G)) / s)
    return {
        "x_words": packed_xT[0],
        "x_scales": packed_xT[1],
        "d_words": packed_dT[0],
        "d_scales": packed_dT[1],
        "gn": (np.random.uniform(0.5, 1.5, (H, 1)) * u[:, None]).astype(np.float32),
        "w1": (n((H, N)) / np.sqrt(H) / u[:, None]).astype(np.float32),
        "offs": striped(np.random.permutation(T)[:S]),
        "kidx": striped8(np.random.randint(0, G, (8, H))),
        "n1": striped8(np.stack([np.random.permutation(S) for _ in range(8)])),
        "n2": striped8(np.stack([np.random.permutation(S) for _ in range(8)])),
        "n3": striped8(np.stack([np.random.permutation(S) for _ in range(8)])),
        "n4": striped8(np.stack([np.random.permutation(S) for _ in range(8)])),
        "n5": striped8(np.stack([np.random.permutation(S) for _ in range(8)])),
    }


def reference(x_words, x_scales, d_words, d_scales, gn, w1, offs, kidx, n1, n2, n3, n4, n5):
    d_kidx = unpack_weight(d_words, d_scales)[np.arange(K)[:, None], runs(kidx, K)]
    xq = unpack_weight(x_words, x_scales)[:, unstriped(offs)]
    s = 0.0625 * (d_kidx.T @ xq)
    z = f64(gn) * (0.75 * (s * (s[np.arange(H)[:, None], runs(n1, H)]) + (s[np.arange(H)[:, None], runs(n2, H)]) * (s[np.arange(H)[:, None], runs(n3, H)])))
    h = mxq(f64(w1), 0, "e4m3").T @ mxq(z, 0, "e4m3")
    sq = (h) ** 2
    return (h[np.arange(N)[:, None], runs(n5, N)]) / (np.sqrt(sq + sq[np.arange(N)[:, None], runs(n4, N)] + 0.25))

@@ -1,0 +1,205 @@
+from contextlib import ExitStack
+
+import concourse.mybir as mybir
+
+K, T, S, N, G, H = 512, 2048, 512, 512, 2048, 512
+FLOPS = 2 * K * H * S + 2 * H * N * S
+
+F32 = mybir.dt.float32
+BF16 = mybir.dt.bfloat16
+I32 = mybir.dt.int32
+U32 = mybir.dt.uint32
+U16 = mybir.dt.uint16
+U8 = mybir.dt.uint8
+FP8X4 = mybir.dt.float8_e4m3fn_x4
+MULT = mybir.AluOpType.mult
+ADD = mybir.AluOpType.add
+ACT = mybir.ActivationFunctionType
+
+P = 128
+PACK = 4
+COL = 16
+Z_CHUNKS = ((0, 384), (384, 512))
+Q_CHUNKS = (((0, 256), (256, 384)), ((384, 512),))
+O_CHUNKS = ((0, 256), (256, 512))
+D_ROW = 14
+D_PLANE_ROW = 12
+D_MOVED = 112
+
+
+def tile_picked_keydotrms_none_p_kernel(
+    tc, x_words, x_scales, d_words, d_scales, gn, w1, offs, kidx, n1, n2, n3, n4, n5, out
+):
+    nc = tc.nc
+    with ExitStack() as ctx:
+        lists = ctx.enter_context(tc.tile_pool(name="lists", bufs=1))
+        keep = ctx.enter_context(tc.tile_pool(name="keep", bufs=1))
+        psum = ctx.enter_context(tc.psum_pool(name="psum", bufs=1))
+
+        def load_list(name, src):
+            t = lists.tile([P, S // COL], U16, name=name)
+            nc.sync.dma_start(t[:], src)
+            return t
+
+        def part(lst, a, b):
+            return lst[:, a // COL : b // COL]
+
+        d_scale_table = keep.tile([P, G], U8, name="d_scale_table")
+        x_scale_table = keep.tile([P, T], U8, name="x_scale_table")
+        d_plane = keep.tile([P, H], U8, name="d_plane", align_bytes=64)
+        nc.gpsimd.memset(d_scale_table[:].bitcast(I32), 0)
+        nc.vector.memset(x_scale_table[:].bitcast(I32), 0)
+        nc.vector.memset(d_plane[:].bitcast(I32), 0)
+        warm = keep.tile([P, 1], F32, name="warm")
+        warm_out = keep.tile([P, 1], F32, name="warm_out")
+        nc.vector.memset(warm[:], 1.0)
+        nc.scalar.activation(warm_out[:], warm[:], ACT.Abs_reciprocal_sqrt)
+
+        kidx_t = load_list("kidx_t", kidx)
+        offs_t = load_list("offs_t", offs)
+        for e in range(PACK):
+            nc.sync.dma_start(
+                d_scale_table[D_ROW + e : P : 32, :].bitcast(I32), d_scales[0, e:16:PACK, :].bitcast(I32)
+            )
+
+        def load_x_scales(e):
+            nc.sync.dma_start(x_scale_table[e:P:32, :].bitcast(I32), x_scales[0, e:16:PACK, :].bitcast(I32))
+
+        load_x_scales(0)
+        d_table = keep.tile([P, G], I32, name="d_table")
+        nc.sync.dma_start(d_table[:], d_words[0].rearrange("p n t -> p (n t)").bitcast(I32))
+        for e in range(1, PACK):
+            load_x_scales(e)
+        x_table = keep.tile([P, T], I32, name="x_table", tag="x_then_w")
+        nc.sync.dma_start(x_table[:], x_words[0].rearrange("p n t -> p (n t)").bitcast(I32))
+        gain_raw = keep.tile([P, PACK], F32, name="gain_raw")
+        nc.scalar.dma_start(gain_raw[:], gn.rearrange("(p t) o -> p (t o)", t=PACK))
+        n2_t = load_list("n2_t", n2)
+        n1_t = load_list("n1_t", n1)
+        n3_t = load_list("n3_t", n3)
+        n4_t = load_list("n4_t", n4)
+        n5_t = load_list("n5_t", n5)
+
+        d_scale_picked = keep.tile([P, H], U8, name="d_scale_picked")
+        d_scale_dealt = keep.tile([P, H], U8, name="d_scale_dealt")
+        nc.vector.tensor_copy(d_scale_picked[:], d_scale_table[:].indirect(kidx_t[:]))
+        nc.vector.tensor_copy(
+            d_scale_dealt[:].rearrange("p (t m) -> p t m", t=PACK),
+            d_scale_picked[:].rearrange("p (m t) -> p t m", t=PACK),
+        )
+        nc.scalar.dma_start(
+            d_plane[D_PLANE_ROW : D_PLANE_ROW + D_MOVED, :].bitcast(I32),
+            d_scale_dealt[D_ROW : D_ROW + D_MOVED, :].bitcast(I32),
+        )
+
+        d_picked = keep.tile([P, H], U32, name="d_picked")
+        d_codes = keep.tile([P, H], U32, name="d_codes", align_bytes=64)
+        nc.vector.tensor_copy(d_picked[:], d_table[:].bitcast(U32).indirect(kidx_t[:]))
+        x_plane = keep.tile([P, S], U8, name="x_plane", align_bytes=64)
+        nc.vector.tensor_copy(x_plane[:], x_scale_table[:].indirect(offs_t[:]))
+        nc.vector.tensor_copy(
+            d_codes[:].rearrange("p (t m) -> p t m", t=PACK),
+            d_picked[:].rearrange("p (m t) -> p t m", t=PACK),
+        )
+        x_codes = keep.tile([P, S], U32, name="x_codes", align_bytes=64)
+        nc.vector.tensor_copy(x_codes[:], x_table[:].bitcast(U32).indirect(offs_t[:]))
+
+        gain = keep.tile([P, PACK], F32, name="gain")
+        nc.vector.tensor_scalar(gain[:], gain_raw[:], 0.75 * 0.0625 * 0.0625, 0.0, MULT, ADD)
+
+        w_raw = keep.tile([P, PACK, N], F32, name="w_raw", tag="x_then_w")
+        nc.sync.dma_start(w_raw[:], w1.rearrange("(p j) c -> p j c", j=PACK))
+
+        raw = []
+        gained = []
+        for t in range(PACK):
+            bank = psum.tile([P, S], F32, name=f"s_bank{t}")
+            cols = slice(t * P, (t + 1) * P)
+            nc.tensor.matmul_mx(
+                out=bank[:],
+                lhsT=d_codes[:, cols].bitcast(FP8X4),
+                lhsT_scale=d_plane[D_PLANE_ROW:P, cols],
+                rhs=x_codes[:].bitcast(FP8X4),
+                rhs_scale=x_plane[:],
+                start=True,
+                stop=True,
+            )
+            gained.append(keep.tile([P, S], F32, name=f"gained{t}"))
+            raw.append(keep.tile([P, S], F32, name=f"raw{t}"))
+            nc.scalar.activation(gained[t][:], bank[:], ACT.Copy, scale=gain[:, t : t + 1])
+            nc.scalar.copy(raw[t][:], bank[:])
+
+        w_grouped = keep.tile([P, N * PACK], BF16, name="w_grouped", align_bytes=64)
+        nc.scalar.copy(
+            w_grouped[:].rearrange("p (t m j) -> p m j t", t=PACK, j=PACK),
+            w_raw[:].rearrange("p j (m t) -> p m j t", t=PACK),
+        )
+        w_codes = keep.tile([P, N], U32, name="w_codes", align_bytes=64)
+        w_plane = keep.tile([P, N], U8, name="w_plane", align_bytes=64)
+
+        h_banks = [psum.tile([P, S], F32, name=f"h_bank{t}") for t in range(PACK)]
+        h = [keep.tile([P, S], F32, name=f"h{t}") for t in range(PACK)]
+        sq = [keep.tile([P, S], F32, name=f"sq{t}") for t in range(PACK)]
+        sq_here = [keep.tile([P, S], F32, name=f"sq_here{t}") for t in range(PACK)]
+
+        for c, (a, b) in enumerate(Z_CHUNKS):
+            w = b - a
+            first = keep.tile([P, PACK, w], F32, name=f"first{c}")
+            second = keep.tile([P, PACK, w], F32, name=f"second{c}")
+            for t in range(PACK):
+                fetched = keep.tile([P, w], F32, name=f"fetched{c}_{t}")
+                nc.vector.tensor_copy(fetched[:], gained[t][:].indirect(part(n2_t, a, b)))
+                nc.vector.tensor_tensor(first[:, t, :], raw[t][:].indirect(part(n1_t, a, b)), gained[t][:, a:b], MULT)
+                nc.vector.tensor_tensor(second[:, t, :], raw[t][:].indirect(part(n3_t, a, b)), fetched[:], MULT)
+            if c == 0:
+                nc.vector.quantize_mx(out=w_codes[:].bitcast(FP8X4), scales=w_plane[:], in_=w_grouped[:])
+            z = keep.tile([P, w * PACK], BF16, name=f"z{c}", align_bytes=64)
+            nc.vector.tensor_tensor(
+                z[:].rearrange("p (g i t) -> p g t i", i=PACK, t=PACK),
+                first[:].rearrange("p t (g i) -> p g t i", i=PACK),
+                second[:].rearrange("p t (g i) -> p g t i", i=PACK),
+                ADD,
+            )
+            for qa, qb in Q_CHUNKS[c]:
+                z_codes = keep.tile([P, qb - qa], U32, name=f"z_codes{qa}", align_bytes=64)
+                z_plane = keep.tile([P, qb - qa], U8, name=f"z_plane{qa}", align_bytes=64)
+                nc.vector.quantize_mx(
+                    out=z_codes[:].bitcast(FP8X4), scales=z_plane[:], in_=z[:, (qa - a) * PACK : (qb - a) * PACK]
+                )
+                for t in range(PACK):
+                    cols = slice(t * P, (t + 1) * P)
+                    nc.tensor.matmul_mx(
+                        out=h_banks[t][:, qa:qb],
+                        lhsT=w_codes[:, cols].bitcast(FP8X4),
+                        lhsT_scale=w_plane[:, cols],
+                        rhs=z_codes[:].bitcast(FP8X4),
+                        rhs_scale=z_plane[:],
+                        start=True,
+                        stop=True,
+                    )
+            for t in range(PACK):
+                nc.scalar.activation(sq[t][:, a:b], h_banks[t][:, a:b], ACT.Square)
+                nc.scalar.activation(sq_here[t][:, a:b], h_banks[t][:, a:b], ACT.Square)
+                nc.scalar.copy(h[t][:, a:b], h_banks[t][:, a:b])
+
+        out_rows = out.rearrange("(p t) j -> p t j", t=PACK)
+        inv = {}
+
+        def denominators(t):
+            for a, b in O_CHUNKS:
+                total = keep.tile([P, b - a], F32, name=f"total{t}_{a}")
+                nc.vector.tensor_tensor(total[:], sq[t][:].indirect(part(n4_t, a, b)), sq_here[t][:, a:b], ADD)
+                inv[t, a] = keep.tile([P, b - a], F32, name=f"inv{t}_{a}")
+                nc.scalar.activation(inv[t, a][:], total[:], ACT.Abs_reciprocal_sqrt, bias=0.25)
+
+        def results(t):
+            for a, b in O_CHUNKS:
+                res = keep.tile([P, b - a], F32, name=f"res{t}_{a}")
+                nc.vector.tensor_tensor(res[:], h[t][:].indirect(part(n5_t, a, b)), inv[t, a][:], MULT)
+                nc.sync.dma_start(out_rows[:, t, a:b], res[:])
+
+        denominators(0)
+        for t in range(1, PACK):
+            denominators(t)
+            results(t - 1)
+        results(PACK - 1)

@@ -1,6 +1,7 @@
 from contextlib import ExitStack
 
 import concourse.mybir as mybir
+from concourse.masks import make_identity
 
 K, T, S, N, G, H = 512, 2048, 512, 512, 2048, 512
 FLOPS = 2 * K * H * S + 2 * H * N * S
@@ -18,13 +19,12 @@ ACT = mybir.ActivationFunctionType
 
 P = 128
 PACK = 4
-COL = 16
-Z_CHUNKS = ((0, 384), (384, 512))
-Q_CHUNKS = (((0, 256), (256, 384)), ((384, 512),))
-O_CHUNKS = ((0, 256), (256, 512))
-D_ROW = 14
-D_PLANE_ROW = 12
-D_MOVED = 112
+GROUP = 16
+QUAD = 32
+BLOCK = 8
+HALVES = ((0, 256), (256, 512))
+TURNED = 384
+Z_CHUNKS = ((0, 256), (256, 384), (384, 512))
 
 
 def tile_picked_keydotrms_none_p_kernel(
@@ -37,97 +37,91 @@ def tile_picked_keydotrms_none_p_kernel(
         psum = ctx.enter_context(tc.psum_pool(name="psum", bufs=1))
 
         def load_list(name, src):
-            t = lists.tile([P, S // COL], U16, name=name)
+            t = lists.tile([P, S // GROUP], U16, name=name)
             nc.sync.dma_start(t[:], src)
             return t
 
         def part(lst, a, b):
-            return lst[:, a // COL : b // COL]
+            return lst[:, a // GROUP : b // GROUP]
 
         d_scale_table = keep.tile([P, G], U8, name="d_scale_table")
         x_scale_table = keep.tile([P, T], U8, name="x_scale_table")
-        d_plane = keep.tile([P, H], U8, name="d_plane", align_bytes=64)
-        nc.gpsimd.memset(d_scale_table[:].bitcast(I32), 0)
-        nc.vector.memset(x_scale_table[:].bitcast(I32), 0)
-        nc.vector.memset(d_plane[:].bitcast(I32), 0)
         warm = keep.tile([P, 1], F32, name="warm")
         warm_out = keep.tile([P, 1], F32, name="warm_out")
+        ident = keep.tile([P, P], F32, name="ident")
+        nc.gpsimd.memset(d_scale_table[:].bitcast(I32), 0)
+        nc.vector.memset(x_scale_table[:].bitcast(I32), 0)
         nc.vector.memset(warm[:], 1.0)
-        nc.scalar.activation(warm_out[:], warm[:], ACT.Abs_reciprocal_sqrt)
+        make_identity(nc, ident[:])
 
         kidx_t = load_list("kidx_t", kidx)
         offs_t = load_list("offs_t", offs)
-        for e in range(PACK):
-            nc.sync.dma_start(
-                d_scale_table[D_ROW + e : P : 32, :].bitcast(I32), d_scales[0, e:16:PACK, :].bitcast(I32)
-            )
-
-        def load_x_scales(e):
-            nc.sync.dma_start(x_scale_table[e:P:32, :].bitcast(I32), x_scales[0, e:16:PACK, :].bitcast(I32))
-
-        load_x_scales(0)
+        nc.sync.dma_start(d_scale_table[0:P:BLOCK, :].bitcast(I32), d_scales[0].bitcast(I32))
         d_table = keep.tile([P, G], I32, name="d_table")
         nc.sync.dma_start(d_table[:], d_words[0].rearrange("p n t -> p (n t)").bitcast(I32))
-        for e in range(1, PACK):
-            load_x_scales(e)
+        for e in range(PACK):
+            nc.scalar.dma_start(x_scale_table[e:P:QUAD, :].bitcast(I32), x_scales[0, e:16:PACK, :].bitcast(I32))
+        nc.scalar.activation(warm_out[:], warm[:], ACT.Abs_reciprocal_sqrt)
         x_table = keep.tile([P, T], I32, name="x_table", tag="x_then_w")
         nc.sync.dma_start(x_table[:], x_words[0].rearrange("p n t -> p (n t)").bitcast(I32))
-        gain_raw = keep.tile([P, PACK], F32, name="gain_raw")
-        nc.scalar.dma_start(gain_raw[:], gn.rearrange("(p t) o -> p (t o)", t=PACK))
+        gain = keep.tile([P, PACK], F32, name="gain")
+        nc.sync.dma_start(gain[:], gn.rearrange("(p t) o -> p (t o)", t=PACK))
         n2_t = load_list("n2_t", n2)
         n1_t = load_list("n1_t", n1)
+
+        d_scale_picked = keep.tile([P, H], U8, name="d_scale_picked")
+        d_plane = keep.tile([P, H], U8, name="d_plane", align_bytes=64)
+        nc.vector.tensor_copy(d_scale_picked[:], d_scale_table[:].indirect(kidx_t[:]))
+        nc.vector.tensor_copy(
+            d_plane[:].rearrange("p (t m) -> p t m", t=PACK),
+            d_scale_picked[:].rearrange("p (m t) -> p t m", t=PACK),
+        )
+        for e in range(1, PACK):
+            nc.sync.dma_start(d_plane[e:P:QUAD, :].bitcast(I32), d_plane[BLOCK * e : P : QUAD, :].bitcast(I32))
+
         n3_t = load_list("n3_t", n3)
         n4_t = load_list("n4_t", n4)
         n5_t = load_list("n5_t", n5)
-
-        d_scale_picked = keep.tile([P, H], U8, name="d_scale_picked")
-        d_scale_dealt = keep.tile([P, H], U8, name="d_scale_dealt")
-        nc.vector.tensor_copy(d_scale_picked[:], d_scale_table[:].indirect(kidx_t[:]))
-        nc.vector.tensor_copy(
-            d_scale_dealt[:].rearrange("p (t m) -> p t m", t=PACK),
-            d_scale_picked[:].rearrange("p (m t) -> p t m", t=PACK),
-        )
-        nc.scalar.dma_start(
-            d_plane[D_PLANE_ROW : D_PLANE_ROW + D_MOVED, :].bitcast(I32),
-            d_scale_dealt[D_ROW : D_ROW + D_MOVED, :].bitcast(I32),
-        )
-
         d_picked = keep.tile([P, H], U32, name="d_picked")
         d_codes = keep.tile([P, H], U32, name="d_codes", align_bytes=64)
-        nc.vector.tensor_copy(d_picked[:], d_table[:].bitcast(U32).indirect(kidx_t[:]))
         x_plane = keep.tile([P, S], U8, name="x_plane", align_bytes=64)
         nc.vector.tensor_copy(x_plane[:], x_scale_table[:].indirect(offs_t[:]))
+        nc.vector.tensor_copy(d_picked[:], d_table[:].bitcast(U32).indirect(kidx_t[:]))
         nc.vector.tensor_copy(
             d_codes[:].rearrange("p (t m) -> p t m", t=PACK),
             d_picked[:].rearrange("p (m t) -> p t m", t=PACK),
         )
         x_codes = keep.tile([P, S], U32, name="x_codes", align_bytes=64)
-        nc.vector.tensor_copy(x_codes[:], x_table[:].bitcast(U32).indirect(offs_t[:]))
-
-        gain = keep.tile([P, PACK], F32, name="gain")
-        nc.vector.tensor_scalar(gain[:], gain_raw[:], 0.75 * 0.0625 * 0.0625, 0.0, MULT, ADD)
+        for a, b in HALVES:
+            nc.vector.tensor_copy(x_codes[:, a:b], x_table[:].bitcast(U32).indirect(part(offs_t, a, b)))
 
         w_raw = keep.tile([P, PACK, N], F32, name="w_raw", tag="x_then_w")
         nc.sync.dma_start(w_raw[:], w1.rearrange("(p j) c -> p j c", j=PACK))
 
-        raw = []
-        gained = []
-        for t in range(PACK):
-            bank = psum.tile([P, S], F32, name=f"s_bank{t}")
+        def product(dst, lhs_codes, lhs_plane, t, rhs_codes, rhs_plane):
             cols = slice(t * P, (t + 1) * P)
             nc.tensor.matmul_mx(
-                out=bank[:],
-                lhsT=d_codes[:, cols].bitcast(FP8X4),
-                lhsT_scale=d_plane[D_PLANE_ROW:P, cols],
-                rhs=x_codes[:].bitcast(FP8X4),
-                rhs_scale=x_plane[:],
+                out=dst,
+                lhsT=lhs_codes[:, cols].bitcast(FP8X4),
+                lhsT_scale=lhs_plane[:, cols],
+                rhs=rhs_codes.bitcast(FP8X4),
+                rhs_scale=rhs_plane,
                 start=True,
                 stop=True,
             )
+
+        raw = []
+        gained = []
+        banks = [psum.tile([P, S], F32, name=f"bank{t}") for t in range(PACK)]
+        h_banks = [psum.tile([P, S], F32, name=f"h_bank{t}") for t in range(PACK)]
+        for t in range(PACK):
             gained.append(keep.tile([P, S], F32, name=f"gained{t}"))
             raw.append(keep.tile([P, S], F32, name=f"raw{t}"))
-            nc.scalar.activation(gained[t][:], bank[:], ACT.Copy, scale=gain[:, t : t + 1])
-            nc.scalar.copy(raw[t][:], bank[:])
+            for a, b in HALVES if t == 0 else ((0, S),):
+                bank = banks[t] if a == 0 else h_banks[0]
+                product(bank[:, a:b], d_codes, d_plane, t, x_codes[:, a:b], x_plane[:, a:b])
+                nc.scalar.activation(gained[t][:, a:b], bank[:, a:b], ACT.Copy, scale=gain[:, t : t + 1])
+                nc.scalar.activation(raw[t][:, a:b], bank[:, a:b], ACT.Copy, scale=0.75 * 0.0625 * 0.0625)
 
         w_grouped = keep.tile([P, N * PACK], BF16, name="w_grouped", align_bytes=64)
         nc.scalar.copy(
@@ -137,69 +131,105 @@ def tile_picked_keydotrms_none_p_kernel(
         w_codes = keep.tile([P, N], U32, name="w_codes", align_bytes=64)
         w_plane = keep.tile([P, N], U8, name="w_plane", align_bytes=64)
 
-        h_banks = [psum.tile([P, S], F32, name=f"h_bank{t}") for t in range(PACK)]
         h = [keep.tile([P, S], F32, name=f"h{t}") for t in range(PACK)]
         sq = [keep.tile([P, S], F32, name=f"sq{t}") for t in range(PACK)]
         sq_here = [keep.tile([P, S], F32, name=f"sq_here{t}") for t in range(PACK)]
 
-        for c, (a, b) in enumerate(Z_CHUNKS):
-            w = b - a
-            first = keep.tile([P, PACK, w], F32, name=f"first{c}")
-            second = keep.tile([P, PACK, w], F32, name=f"second{c}")
+        def terms(a, b, t, first, second, fetched):
+            nc.vector.tensor_copy(fetched, gained[t][:].indirect(part(n2_t, a, b)))
+            nc.vector.tensor_tensor(first, raw[t][:].indirect(part(n1_t, a, b)), gained[t][:, a:b], MULT)
+            nc.vector.tensor_tensor(second, raw[t][:].indirect(part(n3_t, a, b)), fetched, MULT)
+
+        def quantised(a, b, z):
+            z_codes = keep.tile([P, b - a], U32, name=f"z_codes{a}", align_bytes=64)
+            z_plane = keep.tile([P, b - a], U8, name=f"z_plane{a}", align_bytes=64)
+            nc.vector.quantize_mx(out=z_codes[:].bitcast(FP8X4), scales=z_plane[:], in_=z[:])
+            return a, b, z_codes, z_plane
+
+        def second_product(pieces):
             for t in range(PACK):
-                fetched = keep.tile([P, w], F32, name=f"fetched{c}_{t}")
-                nc.vector.tensor_copy(fetched[:], gained[t][:].indirect(part(n2_t, a, b)))
-                nc.vector.tensor_tensor(first[:, t, :], raw[t][:].indirect(part(n1_t, a, b)), gained[t][:, a:b], MULT)
-                nc.vector.tensor_tensor(second[:, t, :], raw[t][:].indirect(part(n3_t, a, b)), fetched[:], MULT)
-            if c == 0:
-                nc.vector.quantize_mx(out=w_codes[:].bitcast(FP8X4), scales=w_plane[:], in_=w_grouped[:])
-            z = keep.tile([P, w * PACK], BF16, name=f"z{c}", align_bytes=64)
-            nc.vector.tensor_tensor(
-                z[:].rearrange("p (g i t) -> p g t i", i=PACK, t=PACK),
-                first[:].rearrange("p t (g i) -> p g t i", i=PACK),
-                second[:].rearrange("p t (g i) -> p g t i", i=PACK),
-                ADD,
-            )
-            for qa, qb in Q_CHUNKS[c]:
-                z_codes = keep.tile([P, qb - qa], U32, name=f"z_codes{qa}", align_bytes=64)
-                z_plane = keep.tile([P, qb - qa], U8, name=f"z_plane{qa}", align_bytes=64)
-                nc.vector.quantize_mx(
-                    out=z_codes[:].bitcast(FP8X4), scales=z_plane[:], in_=z[:, (qa - a) * PACK : (qb - a) * PACK]
-                )
-                for t in range(PACK):
-                    cols = slice(t * P, (t + 1) * P)
-                    nc.tensor.matmul_mx(
-                        out=h_banks[t][:, qa:qb],
-                        lhsT=w_codes[:, cols].bitcast(FP8X4),
-                        lhsT_scale=w_plane[:, cols],
-                        rhs=z_codes[:].bitcast(FP8X4),
-                        rhs_scale=z_plane[:],
-                        start=True,
-                        stop=True,
+                for a, b, z_codes, z_plane in pieces:
+                    product(h_banks[t][:, a:b], w_codes, w_plane, t, z_codes[:], z_plane[:])
+
+        def squares(t, a, b):
+            nc.scalar.activation(sq[t][:, a:b], h_banks[t][:, a:b], ACT.Square)
+            nc.scalar.activation(sq_here[t][:, a:b], h_banks[t][:, a:b], ACT.Square)
+
+        def values(t, a, b):
+            nc.scalar.copy(h[t][:, a:b], h_banks[t][:, a:b])
+
+        firsts = [keep.tile([P, S], F32, name=f"first{i}") for i in range(2)]
+        seconds = [keep.tile([P, S], F32, name=f"second{i}") for i in range(2)]
+        fetcheds = [keep.tile([P, TURNED], F32, name=f"fetched{i}") for i in range(2)]
+        blocks = range(TURNED // P)
+        turned = [banks[j][:].rearrange("q (t p) -> q t p", t=PACK) for j in blocks]
+        for t in range(PACK):
+            first = firsts[t % 2][:, :TURNED]
+            second = seconds[t % 2][:, :TURNED]
+            terms(0, TURNED, t, first, second, fetcheds[t % 2][:])
+            for j in blocks:
+                for term, opens in ((first, True), (second, False)):
+                    nc.tensor.matmul(
+                        turned[j][:, t, :], term[:, j * P : (j + 1) * P], ident[:], start=opens, stop=not opens, is_transpose=True
                     )
-            for t in range(PACK):
-                nc.scalar.activation(sq[t][:, a:b], h_banks[t][:, a:b], ACT.Square)
-                nc.scalar.activation(sq_here[t][:, a:b], h_banks[t][:, a:b], ACT.Square)
-                nc.scalar.copy(h[t][:, a:b], h_banks[t][:, a:b])
+        nc.vector.quantize_mx(out=w_codes[:].bitcast(FP8X4), scales=w_plane[:], in_=w_grouped[:])
+        zs = []
+        for (a, b), bank in zip(Z_CHUNKS[:-1], (banks[3], banks[0])):
+            z = keep.tile([P, (b - a) * PACK], BF16, name=f"z{a}", align_bytes=64)
+            zs.append(z)
+            back = bank[:, : 2 * (b - a)].rearrange("p (j u q) -> p j u q", u=2, q=P)
+            for j in range(a // P, b // P):
+                pairs = w_raw[:, j, : 2 * P]
+                nc.scalar.copy(
+                    pairs.bitcast(BF16).rearrange("q (u p e) -> q u p e", u=2, e=2),
+                    turned[j].rearrange("q (u e) p -> q u p e", u=2),
+                )
+                for u in range(2):
+                    nc.tensor.transpose(back[:, j - a // P, u, :], pairs[:, u * P : (u + 1) * P], ident[:])
+            nc.scalar.copy(
+                z[:].bitcast(F32).rearrange("p (j q u) -> p j q u", q=P, u=2),
+                back.rearrange("p j u q -> p j q u"),
+            )
+        second_product([quantised(a, b, z) for (a, b), z in zip(Z_CHUNKS, zs)])
+        squares(0, 0, TURNED)
+
+        a, b = Z_CHUNKS[-1]
+        first = firsts[0][:].rearrange("p (t j) -> p t j", t=PACK)
+        second = seconds[0][:].rearrange("p (t j) -> p t j", t=PACK)
+        spare = (fetcheds[0], fetcheds[1], fetcheds[0], zs[0][:].bitcast(F32))
+        for t in range(PACK):
+            terms(a, b, t, first[:, t, :], second[:, t, :], spare[t][:, : b - a])
+        z = keep.tile([P, (b - a) * PACK], BF16, name=f"z{a}", align_bytes=64)
+        nc.vector.tensor_tensor(
+            z[:].rearrange("p (g i t) -> p g t i", i=PACK, t=PACK),
+            first.rearrange("p t (g i) -> p g t i", i=PACK),
+            second.rearrange("p t (g i) -> p g t i", i=PACK),
+            ADD,
+        )
+        second_product([quantised(a, b, z)])
 
         out_rows = out.rearrange("(p t) j -> p t j", t=PACK)
         inv = {}
 
         def denominators(t):
-            for a, b in O_CHUNKS:
+            for a, b in HALVES:
                 total = keep.tile([P, b - a], F32, name=f"total{t}_{a}")
                 nc.vector.tensor_tensor(total[:], sq[t][:].indirect(part(n4_t, a, b)), sq_here[t][:, a:b], ADD)
                 inv[t, a] = keep.tile([P, b - a], F32, name=f"inv{t}_{a}")
                 nc.scalar.activation(inv[t, a][:], total[:], ACT.Abs_reciprocal_sqrt, bias=0.25)
+                if a == 0:
+                    values(t, 0, S)
 
         def results(t):
-            for a, b in O_CHUNKS:
+            for a, b in HALVES:
                 res = keep.tile([P, b - a], F32, name=f"res{t}_{a}")
                 nc.vector.tensor_tensor(res[:], h[t][:].indirect(part(n5_t, a, b)), inv[t, a][:], MULT)
                 nc.sync.dma_start(out_rows[:, t, a:b], res[:])
 
-        denominators(0)
-        for t in range(1, PACK):
-            denominators(t)
-            results(t - 1)
-        results(PACK - 1)
+        for pair in ((0, 1), (2, 3)):
+            for t in pair:
+                squares(t, TURNED if t == 0 else 0, S)
+            for t in pair:
+                denominators(t)
+            for t in pair:
+                results(t)

@@ -21,7 +21,6 @@ P = 128
 PACK = 4
 GROUP = 16
 QUAD = 32
-BLOCK = 8
 HALVES = ((0, 256), (256, 512))
 TURNED = 384
 Z_CHUNKS = ((0, 256), (256, 384), (384, 512))
@@ -49,14 +48,15 @@ def tile_picked_keydotrms_none_p_kernel(
         warm = keep.tile([P, 1], F32, name="warm")
         warm_out = keep.tile([P, 1], F32, name="warm_out")
         ident = keep.tile([P, P], F32, name="ident")
-        nc.gpsimd.memset(d_scale_table[:].bitcast(I32), 0)
-        nc.vector.memset(x_scale_table[:].bitcast(I32), 0)
-        nc.vector.memset(warm[:], 1.0)
+        nc.vector.memset(d_scale_table[:].bitcast(I32), 0)
+        nc.gpsimd.memset(x_scale_table[:].bitcast(I32), 0)
+        nc.gpsimd.memset(warm[:], 1.0)
         make_identity(nc, ident[:])
 
         kidx_t = load_list("kidx_t", kidx)
         offs_t = load_list("offs_t", offs)
-        nc.sync.dma_start(d_scale_table[0:P:BLOCK, :].bitcast(I32), d_scales[0].bitcast(I32))
+        for u in range(2):
+            nc.sync.dma_start(d_scale_table[u:P:GROUP, :].bitcast(I32), d_scales[0, u:16:2, :].bitcast(I32))
         d_table = keep.tile([P, G], I32, name="d_table")
         nc.sync.dma_start(d_table[:], d_words[0].rearrange("p n t -> p (n t)").bitcast(I32))
         for e in range(PACK):
@@ -69,22 +69,22 @@ def tile_picked_keydotrms_none_p_kernel(
         n2_t = load_list("n2_t", n2)
         n1_t = load_list("n1_t", n1)
 
-        d_scale_picked = keep.tile([P, H], U8, name="d_scale_picked")
+        d_scale_picked = keep.tile([P, H], U8, name="d_scale_picked", align_bytes=64)
         d_plane = keep.tile([P, H], U8, name="d_plane", align_bytes=64)
         nc.vector.tensor_copy(d_scale_picked[:], d_scale_table[:].indirect(kidx_t[:]))
         nc.vector.tensor_copy(
             d_plane[:].rearrange("p (t m) -> p t m", t=PACK),
             d_scale_picked[:].rearrange("p (m t) -> p t m", t=PACK),
         )
-        for e in range(1, PACK):
-            nc.sync.dma_start(d_plane[e:P:QUAD, :].bitcast(I32), d_plane[BLOCK * e : P : QUAD, :].bitcast(I32))
+        for u in range(2):
+            nc.scalar.dma_start(d_plane[2 + u : P : QUAD, :].bitcast(I32), d_plane[GROUP + u : P : QUAD, :].bitcast(I32))
 
         n3_t = load_list("n3_t", n3)
         n4_t = load_list("n4_t", n4)
         n5_t = load_list("n5_t", n5)
         d_picked = keep.tile([P, H], U32, name="d_picked")
         d_codes = keep.tile([P, H], U32, name="d_codes", align_bytes=64)
-        x_plane = keep.tile([P, S], U8, name="x_plane", align_bytes=64)
+        x_plane = d_scale_picked
         nc.vector.tensor_copy(x_plane[:], x_scale_table[:].indirect(offs_t[:]))
         nc.vector.tensor_copy(d_picked[:], d_table[:].bitcast(U32).indirect(kidx_t[:]))
         nc.vector.tensor_copy(
@@ -125,8 +125,8 @@ def tile_picked_keydotrms_none_p_kernel(
 
         w_grouped = keep.tile([P, N * PACK], BF16, name="w_grouped", align_bytes=64)
         nc.scalar.copy(
-            w_grouped[:].rearrange("p (t m j) -> p m j t", t=PACK, j=PACK),
-            w_raw[:].rearrange("p j (m t) -> p m j t", t=PACK),
+            w_grouped[:].rearrange("p (t m j) -> p t m j", t=PACK, j=PACK),
+            w_raw[:].rearrange("p j (m t) -> p t m j", t=PACK),
         )
         w_codes = keep.tile([P, N], U32, name="w_codes", align_bytes=64)
         w_plane = keep.tile([P, N], U8, name="w_plane", align_bytes=64)
@@ -135,10 +135,13 @@ def tile_picked_keydotrms_none_p_kernel(
         sq = [keep.tile([P, S], F32, name=f"sq{t}") for t in range(PACK)]
         sq_here = [keep.tile([P, S], F32, name=f"sq_here{t}") for t in range(PACK)]
 
-        def terms(a, b, t, first, second, fetched):
+        def terms(a, b, t, first, second, fetched, step):
             nc.vector.tensor_copy(fetched, gained[t][:].indirect(part(n2_t, a, b)))
             nc.vector.tensor_tensor(first, raw[t][:].indirect(part(n1_t, a, b)), gained[t][:, a:b], MULT)
-            nc.vector.tensor_tensor(second, raw[t][:].indirect(part(n3_t, a, b)), fetched, MULT)
+            for c in range(0, b - a, step):
+                nc.vector.tensor_tensor(
+                    second[:, c : c + step], raw[t][:].indirect(part(n3_t, a + c, a + c + step)), fetched[:, c : c + step], MULT
+                )
 
         def quantised(a, b, z):
             z_codes = keep.tile([P, b - a], U32, name=f"z_codes{a}", align_bytes=64)
@@ -158,15 +161,15 @@ def tile_picked_keydotrms_none_p_kernel(
         def values(t, a, b):
             nc.scalar.copy(h[t][:, a:b], h_banks[t][:, a:b])
 
-        firsts = [keep.tile([P, S], F32, name=f"first{i}") for i in range(2)]
-        seconds = [keep.tile([P, S], F32, name=f"second{i}") for i in range(2)]
+        firsts = [keep.tile([P, S], F32, name=f"first{i}") for i in range(PACK)]
+        seconds = [keep.tile([P, S], F32, name=f"second{i}") for i in range(PACK)]
         fetcheds = [keep.tile([P, TURNED], F32, name=f"fetched{i}") for i in range(2)]
         blocks = range(TURNED // P)
         turned = [banks[j][:].rearrange("q (t p) -> q t p", t=PACK) for j in blocks]
         for t in range(PACK):
-            first = firsts[t % 2][:, :TURNED]
-            second = seconds[t % 2][:, :TURNED]
-            terms(0, TURNED, t, first, second, fetcheds[t % 2][:])
+            first = firsts[t][:, :TURNED]
+            second = seconds[t][:, :TURNED]
+            terms(0, TURNED, t, first, second, fetcheds[t % 2][:], P if t == PACK - 1 else TURNED)
             for j in blocks:
                 for term, opens in ((first, True), (second, False)):
                     nc.tensor.matmul(
@@ -194,11 +197,11 @@ def tile_picked_keydotrms_none_p_kernel(
         squares(0, 0, TURNED)
 
         a, b = Z_CHUNKS[-1]
-        first = firsts[0][:].rearrange("p (t j) -> p t j", t=PACK)
-        second = seconds[0][:].rearrange("p (t j) -> p t j", t=PACK)
+        first = firsts[2][:].rearrange("p (t j) -> p t j", t=PACK)
+        second = seconds[2][:].rearrange("p (t j) -> p t j", t=PACK)
         spare = (fetcheds[0], fetcheds[1], fetcheds[0], zs[0][:].bitcast(F32))
         for t in range(PACK):
-            terms(a, b, t, first[:, t, :], second[:, t, :], spare[t][:, : b - a])
+            terms(a, b, t, first[:, t, :], second[:, t, :], spare[t][:, : b - a], P)
         z = keep.tile([P, (b - a) * PACK], BF16, name=f"z{a}", align_bytes=64)
         nc.vector.tensor_tensor(
             z[:].rearrange("p (g i t) -> p g t i", i=PACK, t=PACK),

@@ -154,9 +154,8 @@ def tile_picked_keydotrms_none_p_kernel(
                 for a, b, z_codes, z_plane in pieces:
                     product(h_banks[t][:, a:b], w_codes, w_plane, t, z_codes[:], z_plane[:])
 
-        def squares(t, a, b):
-            nc.scalar.activation(sq[t][:, a:b], h_banks[t][:, a:b], ACT.Square)
-            nc.scalar.activation(sq_here[t][:, a:b], h_banks[t][:, a:b], ACT.Square)
+        def square(dst, t, a, b):
+            nc.scalar.activation(dst[t][:, a:b], h_banks[t][:, a:b], ACT.Square)
 
         def values(t, a, b):
             nc.scalar.copy(h[t][:, a:b], h_banks[t][:, a:b])
@@ -194,10 +193,12 @@ def tile_picked_keydotrms_none_p_kernel(
                 back.rearrange("p j u q -> p j q u"),
             )
         second_product([quantised(a, b, z) for (a, b), z in zip(Z_CHUNKS, zs)])
-        squares(0, 0, TURNED)
+        square(sq, 0, 0, TURNED)
+        square(sq_here, 0, 0, TURNED)
+        square(sq, 1, 0, TURNED)
 
         a, b = Z_CHUNKS[-1]
-        first = firsts[2][:].rearrange("p (t j) -> p t j", t=PACK)
+        first = firsts[3][:].rearrange("p (t j) -> p t j", t=PACK)
         second = seconds[2][:].rearrange("p (t j) -> p t j", t=PACK)
         spare = (fetcheds[0], fetcheds[1], fetcheds[0], zs[0][:].bitcast(F32))
         for t in range(PACK):
@@ -212,26 +213,26 @@ def tile_picked_keydotrms_none_p_kernel(
         second_product([quantised(a, b, z)])
 
         out_rows = out.rearrange("(p t) j -> p t j", t=PACK)
-        inv = {}
+        inv = [keep.tile([P, S], F32, name=f"inv{t}") for t in range(PACK)]
 
         def denominators(t):
             for a, b in HALVES:
                 total = keep.tile([P, b - a], F32, name=f"total{t}_{a}")
                 nc.vector.tensor_tensor(total[:], sq[t][:].indirect(part(n4_t, a, b)), sq_here[t][:, a:b], ADD)
-                inv[t, a] = keep.tile([P, b - a], F32, name=f"inv{t}_{a}")
-                nc.scalar.activation(inv[t, a][:], total[:], ACT.Abs_reciprocal_sqrt, bias=0.25)
+                nc.scalar.activation(inv[t][:, a:b], total[:], ACT.Abs_reciprocal_sqrt, bias=0.25)
                 if a == 0:
                     values(t, 0, S)
 
         def results(t):
-            for a, b in HALVES:
+            for a, b in Z_CHUNKS if t == PACK - 1 else HALVES:
                 res = keep.tile([P, b - a], F32, name=f"res{t}_{a}")
-                nc.vector.tensor_tensor(res[:], h[t][:].indirect(part(n5_t, a, b)), inv[t, a][:], MULT)
+                nc.vector.tensor_tensor(res[:], h[t][:].indirect(part(n5_t, a, b)), inv[t][:, a:b], MULT)
                 nc.sync.dma_start(out_rows[:, t, a:b], res[:])
 
         for pair in ((0, 1), (2, 3)):
             for t in pair:
-                squares(t, TURNED if t == 0 else 0, S)
+                square(sq, t, TURNED if t < 2 else 0, S)
+                square(sq_here, t, TURNED if t < 1 else 0, S)
             for t in pair:
                 denominators(t)
             for t in pair:

@@ -21,9 +21,14 @@ P = 128
 PACK = 4
 GROUP = 16
 QUAD = 32
-HALVES = ((0, 256), (256, 512))
+SCALE_ROWS = K // 32
+LAST = PACK - 1
+
+WHOLE = ((0, S),)
+HALVES = ((0, S // 2), (S // 2, S))
 TURNED = 384
-Z_CHUNKS = ((0, 256), (256, 384), (384, 512))
+TURNED_PIECES = ((0, 256), (256, TURNED))
+TAPER = TURNED_PIECES + ((TURNED, S),)
 
 
 def tile_picked_keydotrms_none_p_kernel(
@@ -36,32 +41,37 @@ def tile_picked_keydotrms_none_p_kernel(
         psum = ctx.enter_context(tc.psum_pool(name="psum", bufs=1))
 
         def load_list(name, src):
-            t = lists.tile([P, S // GROUP], U16, name=name)
-            nc.sync.dma_start(t[:], src)
-            return t
+            list_tile = lists.tile([P, S // GROUP], U16, name=name)
+            nc.sync.dma_start(list_tile[:], src)
+            return list_tile
 
-        def part(lst, a, b):
-            return lst[:, a // GROUP : b // GROUP]
+        def entries(list_tile, a, b):
+            return list_tile[:, a // GROUP : b // GROUP]
 
         d_scale_table = keep.tile([P, G], U8, name="d_scale_table")
         x_scale_table = keep.tile([P, T], U8, name="x_scale_table")
-        warm = keep.tile([P, 1], F32, name="warm")
-        warm_out = keep.tile([P, 1], F32, name="warm_out")
+        sixteen = keep.tile([P, 1], F32, name="sixteen")
+        quarter = keep.tile([P, 1], F32, name="quarter")
         ident = keep.tile([P, P], F32, name="ident")
         nc.vector.memset(d_scale_table[:].bitcast(I32), 0)
         nc.gpsimd.memset(x_scale_table[:].bitcast(I32), 0)
-        nc.gpsimd.memset(warm[:], 1.0)
+        nc.gpsimd.memset(sixteen[:], 16.0)
         make_identity(nc, ident[:])
+
+        sq_window = [keep.tile([P, 2 * S], F32, name=f"sq_window{t}") for t in range(PACK)]
+        sq = [window[:, :S] for window in sq_window]
+        for window in sq_window:
+            nc.vector.memset(window[:, S:], 0.0)
 
         kidx_t = load_list("kidx_t", kidx)
         offs_t = load_list("offs_t", offs)
         for u in range(2):
-            nc.sync.dma_start(d_scale_table[u:P:GROUP, :].bitcast(I32), d_scales[0, u:16:2, :].bitcast(I32))
+            nc.sync.dma_start(d_scale_table[u:P:GROUP, :].bitcast(I32), d_scales[0, u:SCALE_ROWS:2, :].bitcast(I32))
         d_table = keep.tile([P, G], I32, name="d_table")
         nc.sync.dma_start(d_table[:], d_words[0].rearrange("p n t -> p (n t)").bitcast(I32))
         for e in range(PACK):
-            nc.scalar.dma_start(x_scale_table[e:P:QUAD, :].bitcast(I32), x_scales[0, e:16:PACK, :].bitcast(I32))
-        nc.scalar.activation(warm_out[:], warm[:], ACT.Abs_reciprocal_sqrt)
+            nc.scalar.dma_start(x_scale_table[e:P:QUAD, :].bitcast(I32), x_scales[0, e:SCALE_ROWS:PACK, :].bitcast(I32))
+        nc.scalar.activation(quarter[:], sixteen[:], ACT.Abs_reciprocal_sqrt)
         x_table = keep.tile([P, T], I32, name="x_table", tag="x_then_w")
         nc.sync.dma_start(x_table[:], x_words[0].rearrange("p n t -> p (n t)").bitcast(I32))
         gain = keep.tile([P, PACK], F32, name="gain")
@@ -69,12 +79,12 @@ def tile_picked_keydotrms_none_p_kernel(
         n2_t = load_list("n2_t", n2)
         n1_t = load_list("n1_t", n1)
 
-        d_scale_picked = keep.tile([P, H], U8, name="d_scale_picked", align_bytes=64)
+        picked_bytes = keep.tile([P, H], U8, name="picked_bytes", align_bytes=64)
         d_plane = keep.tile([P, H], U8, name="d_plane", align_bytes=64)
-        nc.vector.tensor_copy(d_scale_picked[:], d_scale_table[:].indirect(kidx_t[:]))
+        nc.vector.tensor_copy(picked_bytes[:], d_scale_table[:].indirect(kidx_t[:]))
         nc.vector.tensor_copy(
             d_plane[:].rearrange("p (t m) -> p t m", t=PACK),
-            d_scale_picked[:].rearrange("p (m t) -> p t m", t=PACK),
+            picked_bytes[:].rearrange("p (m t) -> p t m", t=PACK),
         )
         for u in range(2):
             nc.scalar.dma_start(d_plane[2 + u : P : QUAD, :].bitcast(I32), d_plane[GROUP + u : P : QUAD, :].bitcast(I32))
@@ -82,10 +92,10 @@ def tile_picked_keydotrms_none_p_kernel(
         n3_t = load_list("n3_t", n3)
         n4_t = load_list("n4_t", n4)
         n5_t = load_list("n5_t", n5)
+
         d_picked = keep.tile([P, H], U32, name="d_picked")
         d_codes = keep.tile([P, H], U32, name="d_codes", align_bytes=64)
-        x_plane = d_scale_picked
-        nc.vector.tensor_copy(x_plane[:], x_scale_table[:].indirect(offs_t[:]))
+        nc.vector.tensor_copy(picked_bytes[:], x_scale_table[:].indirect(offs_t[:]))
         nc.vector.tensor_copy(d_picked[:], d_table[:].bitcast(U32).indirect(kidx_t[:]))
         nc.vector.tensor_copy(
             d_codes[:].rearrange("p (t m) -> p t m", t=PACK),
@@ -93,7 +103,7 @@ def tile_picked_keydotrms_none_p_kernel(
         )
         x_codes = keep.tile([P, S], U32, name="x_codes", align_bytes=64)
         for a, b in HALVES:
-            nc.vector.tensor_copy(x_codes[:, a:b], x_table[:].bitcast(U32).indirect(part(offs_t, a, b)))
+            nc.vector.tensor_copy(x_codes[:, a:b], x_table[:].bitcast(U32).indirect(entries(offs_t, a, b)))
 
         w_raw = keep.tile([P, PACK, N], F32, name="w_raw", tag="x_then_w")
         nc.sync.dma_start(w_raw[:], w1.rearrange("(p j) c -> p j c", j=PACK))
@@ -110,18 +120,18 @@ def tile_picked_keydotrms_none_p_kernel(
                 stop=True,
             )
 
-        raw = []
+        scaled = []
         gained = []
         banks = [psum.tile([P, S], F32, name=f"bank{t}") for t in range(PACK)]
         h_banks = [psum.tile([P, S], F32, name=f"h_bank{t}") for t in range(PACK)]
         for t in range(PACK):
             gained.append(keep.tile([P, S], F32, name=f"gained{t}"))
-            raw.append(keep.tile([P, S], F32, name=f"raw{t}"))
-            for a, b in HALVES if t == 0 else ((0, S),):
+            scaled.append(keep.tile([P, S], F32, name=f"scaled{t}"))
+            for a, b in HALVES if t == 0 else WHOLE:
                 bank = banks[t] if a == 0 else h_banks[0]
-                product(bank[:, a:b], d_codes, d_plane, t, x_codes[:, a:b], x_plane[:, a:b])
+                product(bank[:, a:b], d_codes, d_plane, t, x_codes[:, a:b], picked_bytes[:, a:b])
                 nc.scalar.activation(gained[t][:, a:b], bank[:, a:b], ACT.Copy, scale=gain[:, t : t + 1])
-                nc.scalar.activation(raw[t][:, a:b], bank[:, a:b], ACT.Copy, scale=0.75 * 0.0625 * 0.0625)
+                nc.scalar.activation(scaled[t][:, a:b], bank[:, a:b], ACT.Copy, scale=0.75 * 0.0625 * 0.0625)
 
         w_grouped = keep.tile([P, N * PACK], BF16, name="w_grouped", align_bytes=64)
         nc.scalar.copy(
@@ -131,17 +141,16 @@ def tile_picked_keydotrms_none_p_kernel(
         w_codes = keep.tile([P, N], U32, name="w_codes", align_bytes=64)
         w_plane = keep.tile([P, N], U8, name="w_plane", align_bytes=64)
 
-        h = [keep.tile([P, S], F32, name=f"h{t}") for t in range(PACK)]
-        sq = [keep.tile([P, S], F32, name=f"sq{t}") for t in range(PACK)]
-        sq_here = [keep.tile([P, S], F32, name=f"sq_here{t}") for t in range(PACK)]
+        h_window = [keep.tile([P, 2 * S], F32, name=f"h_window{t}") for t in range(PACK)]
+        h = [window[:, :S] for window in h_window]
+        sq_here = [window[:, S:] for window in h_window]
 
         def terms(a, b, t, first, second, fetched, step):
-            nc.vector.tensor_copy(fetched, gained[t][:].indirect(part(n2_t, a, b)))
-            nc.vector.tensor_tensor(first, raw[t][:].indirect(part(n1_t, a, b)), gained[t][:, a:b], MULT)
+            nc.vector.tensor_copy(fetched, gained[t][:].indirect(entries(n2_t, a, b)))
+            nc.vector.tensor_tensor(first, scaled[t][:].indirect(entries(n1_t, a, b)), gained[t][:, a:b], MULT)
             for c in range(0, b - a, step):
-                nc.vector.tensor_tensor(
-                    second[:, c : c + step], raw[t][:].indirect(part(n3_t, a + c, a + c + step)), fetched[:, c : c + step], MULT
-                )
+                looked_up = scaled[t][:].indirect(entries(n3_t, a + c, a + c + step))
+                nc.vector.tensor_tensor(second[:, c : c + step], looked_up, fetched[:, c : c + step], MULT)
 
         def quantised(a, b, z):
             z_codes = keep.tile([P, b - a], U32, name=f"z_codes{a}", align_bytes=64)
@@ -157,28 +166,25 @@ def tile_picked_keydotrms_none_p_kernel(
         def square(dst, t, a, b):
             nc.scalar.activation(dst[t][:, a:b], h_banks[t][:, a:b], ACT.Square)
 
-        def values(t, a, b):
-            nc.scalar.copy(h[t][:, a:b], h_banks[t][:, a:b])
-
-        firsts = [keep.tile([P, S], F32, name=f"first{i}") for i in range(PACK)]
-        seconds = [keep.tile([P, S], F32, name=f"second{i}") for i in range(PACK)]
+        firsts = [keep.tile([P, S], F32, name=f"first{t}") for t in range(PACK)]
+        seconds = [keep.tile([P, S], F32, name=f"second{t}") for t in range(PACK)]
         fetcheds = [keep.tile([P, TURNED], F32, name=f"fetched{i}") for i in range(2)]
         blocks = range(TURNED // P)
         turned = [banks[j][:].rearrange("q (t p) -> q t p", t=PACK) for j in blocks]
         for t in range(PACK):
             first = firsts[t][:, :TURNED]
             second = seconds[t][:, :TURNED]
-            terms(0, TURNED, t, first, second, fetcheds[t % 2][:], P if t == PACK - 1 else TURNED)
+            terms(0, TURNED, t, first, second, fetcheds[t % 2][:], P if t == LAST else TURNED)
             for j in blocks:
                 for term, opens in ((first, True), (second, False)):
-                    nc.tensor.matmul(
-                        turned[j][:, t, :], term[:, j * P : (j + 1) * P], ident[:], start=opens, stop=not opens, is_transpose=True
-                    )
+                    block = term[:, j * P : (j + 1) * P]
+                    nc.tensor.matmul(turned[j][:, t, :], block, ident[:], start=opens, stop=not opens, is_transpose=True)
         nc.vector.quantize_mx(out=w_codes[:].bitcast(FP8X4), scales=w_plane[:], in_=w_grouped[:])
-        zs = []
-        for (a, b), bank in zip(Z_CHUNKS[:-1], (banks[3], banks[0])):
+
+        turned_z = []
+        for (a, b), bank in zip(TURNED_PIECES, (banks[len(blocks)], banks[0])):
             z = keep.tile([P, (b - a) * PACK], BF16, name=f"z{a}", align_bytes=64)
-            zs.append(z)
+            turned_z.append(z)
             back = bank[:, : 2 * (b - a)].rearrange("p (j u q) -> p j u q", u=2, q=P)
             for j in range(a // P, b // P):
                 pairs = w_raw[:, j, : 2 * P]
@@ -192,48 +198,46 @@ def tile_picked_keydotrms_none_p_kernel(
                 z[:].bitcast(F32).rearrange("p (j q u) -> p j q u", q=P, u=2),
                 back.rearrange("p j u q -> p j q u"),
             )
-        second_product([quantised(a, b, z) for (a, b), z in zip(Z_CHUNKS, zs)])
-        square(sq, 0, 0, TURNED)
-        square(sq_here, 0, 0, TURNED)
-        square(sq, 1, 0, TURNED)
+        second_product([quantised(a, b, z) for (a, b), z in zip(TURNED_PIECES, turned_z)])
 
-        a, b = Z_CHUNKS[-1]
-        first = firsts[3][:].rearrange("p (t j) -> p t j", t=PACK)
-        second = seconds[2][:].rearrange("p (t j) -> p t j", t=PACK)
-        spare = (fetcheds[0], fetcheds[1], fetcheds[0], zs[0][:].bitcast(F32))
+        for dst, t in ((sq, 0), (sq_here, 0), (sq, 1)):
+            square(dst, t, 0, TURNED)
+
+        first = firsts[LAST][:].rearrange("p (t j) -> p t j", t=PACK)
+        second = seconds[LAST - 1][:].rearrange("p (t j) -> p t j", t=PACK)
         for t in range(PACK):
-            terms(a, b, t, first[:, t, :], second[:, t, :], spare[t][:, : b - a], P)
-        z = keep.tile([P, (b - a) * PACK], BF16, name=f"z{a}", align_bytes=64)
+            fetched = turned_z[0][:].bitcast(F32) if t == LAST else fetcheds[t % 2]
+            terms(TURNED, S, t, first[:, t, :], second[:, t, :], fetched[:, : S - TURNED], S - TURNED)
+        z = keep.tile([P, (S - TURNED) * PACK], BF16, name=f"z{TURNED}", align_bytes=64)
         nc.vector.tensor_tensor(
             z[:].rearrange("p (g i t) -> p g t i", i=PACK, t=PACK),
             first.rearrange("p t (g i) -> p g t i", i=PACK),
             second.rearrange("p t (g i) -> p g t i", i=PACK),
             ADD,
         )
-        second_product([quantised(a, b, z)])
+        second_product([quantised(TURNED, S, z)])
 
         out_rows = out.rearrange("(p t) j -> p t j", t=PACK)
         inv = [keep.tile([P, S], F32, name=f"inv{t}") for t in range(PACK)]
 
         def denominators(t):
-            for a, b in HALVES:
+            for a, b in HALVES if t == 0 else WHOLE:
                 total = keep.tile([P, b - a], F32, name=f"total{t}_{a}")
-                nc.vector.tensor_tensor(total[:], sq[t][:].indirect(part(n4_t, a, b)), sq_here[t][:, a:b], ADD)
-                nc.scalar.activation(inv[t][:, a:b], total[:], ACT.Abs_reciprocal_sqrt, bias=0.25)
-                if a == 0:
-                    values(t, 0, S)
+                nc.vector.tensor_tensor(total[:], sq_window[t][:].indirect(entries(n4_t, a, b)), sq_here[t][:, a:b], ADD)
+                nc.scalar.activation(inv[t][:, a:b], total[:], ACT.Abs_reciprocal_sqrt, bias=quarter[:])
 
         def results(t):
-            for a, b in Z_CHUNKS if t == PACK - 1 else HALVES:
+            for a, b in TAPER if t == LAST else WHOLE:
                 res = keep.tile([P, b - a], F32, name=f"res{t}_{a}")
-                nc.vector.tensor_tensor(res[:], h[t][:].indirect(part(n5_t, a, b)), inv[t][:, a:b], MULT)
+                nc.vector.tensor_tensor(res[:], h_window[t][:].indirect(entries(n5_t, a, b)), inv[t][:, a:b], MULT)
                 nc.sync.dma_start(out_rows[:, t, a:b], res[:])
 
         for pair in ((0, 1), (2, 3)):
             for t in pair:
-                square(sq, t, TURNED if t < 2 else 0, S)
-                square(sq_here, t, TURNED if t < 1 else 0, S)
+                square(sq, t, TURNED if t <= 1 else 0, S)
+                square(sq_here, t, TURNED if t == 0 else 0, S)
             for t in pair:
+                nc.scalar.copy(h[t], h_banks[t][:])
                 denominators(t)
             for t in pair:
                 results(t)

from contextlib import ExitStack

import concourse.mybir as mybir
from concourse.masks import make_identity

K, T, S, N, G, H = 512, 2048, 512, 512, 2048, 512
FLOPS = 2 * K * H * S + 2 * H * N * S

F32 = mybir.dt.float32
BF16 = mybir.dt.bfloat16
I32 = mybir.dt.int32
U32 = mybir.dt.uint32
U16 = mybir.dt.uint16
U8 = mybir.dt.uint8
FP8X4 = mybir.dt.float8_e4m3fn_x4
MULT = mybir.AluOpType.mult
ADD = mybir.AluOpType.add
ACT = mybir.ActivationFunctionType

P = 128
PACK = 4
GROUP = 16
QUAD = 32
SCALE_ROWS = K // 32
LAST = PACK - 1

WHOLE = ((0, S),)
HALVES = ((0, S // 2), (S // 2, S))
TURNED = 384
TURNED_PIECES = ((0, 256), (256, TURNED))
TAPER = TURNED_PIECES + ((TURNED, S),)


def tile_picked_keydotrms_none_p_kernel(
    tc, x_words, x_scales, d_words, d_scales, gn, w1, offs, kidx, n1, n2, n3, n4, n5, out
):
    nc = tc.nc
    with ExitStack() as ctx:
        lists = ctx.enter_context(tc.tile_pool(name="lists", bufs=1))
        keep = ctx.enter_context(tc.tile_pool(name="keep", bufs=1))
        psum = ctx.enter_context(tc.psum_pool(name="psum", bufs=1))

        def load_list(name, src):
            list_tile = lists.tile([P, S // GROUP], U16, name=name)
            nc.sync.dma_start(list_tile[:], src)
            return list_tile

        def entries(list_tile, a, b):
            return list_tile[:, a // GROUP : b // GROUP]

        d_scale_table = keep.tile([P, G], U8, name="d_scale_table")
        x_scale_table = keep.tile([P, T], U8, name="x_scale_table")
        sixteen = keep.tile([P, 1], F32, name="sixteen")
        quarter = keep.tile([P, 1], F32, name="quarter")
        ident = keep.tile([P, P], F32, name="ident")
        nc.vector.memset(d_scale_table[:].bitcast(I32), 0)
        nc.gpsimd.memset(x_scale_table[:].bitcast(I32), 0)
        nc.gpsimd.memset(sixteen[:], 16.0)
        make_identity(nc, ident[:])

        sq_window = [keep.tile([P, 2 * S], F32, name=f"sq_window{t}") for t in range(PACK)]
        sq = [window[:, :S] for window in sq_window]
        for window in sq_window:
            nc.vector.memset(window[:, S:], 0.0)

        kidx_t = load_list("kidx_t", kidx)
        offs_t = load_list("offs_t", offs)
        for u in range(2):
            nc.sync.dma_start(d_scale_table[u:P:GROUP, :].bitcast(I32), d_scales[0, u:SCALE_ROWS:2, :].bitcast(I32))
        d_table = keep.tile([P, G], I32, name="d_table")
        nc.sync.dma_start(d_table[:], d_words[0].rearrange("p n t -> p (n t)").bitcast(I32))
        for e in range(PACK):
            nc.scalar.dma_start(x_scale_table[e:P:QUAD, :].bitcast(I32), x_scales[0, e:SCALE_ROWS:PACK, :].bitcast(I32))
        nc.scalar.activation(quarter[:], sixteen[:], ACT.Abs_reciprocal_sqrt)
        x_table = keep.tile([P, T], I32, name="x_table", tag="x_then_w")
        nc.sync.dma_start(x_table[:], x_words[0].rearrange("p n t -> p (n t)").bitcast(I32))
        gain = keep.tile([P, PACK], F32, name="gain")
        nc.sync.dma_start(gain[:], gn.rearrange("(p t) o -> p (t o)", t=PACK))
        n2_t = load_list("n2_t", n2)
        n1_t = load_list("n1_t", n1)

        picked_bytes = keep.tile([P, H], U8, name="picked_bytes", align_bytes=64)
        d_plane = keep.tile([P, H], U8, name="d_plane", align_bytes=64)
        nc.vector.tensor_copy(picked_bytes[:], d_scale_table[:].indirect(kidx_t[:]))
        nc.vector.tensor_copy(
            d_plane[:].rearrange("p (t m) -> p t m", t=PACK),
            picked_bytes[:].rearrange("p (m t) -> p t m", t=PACK),
        )
        for u in range(2):
            nc.scalar.dma_start(d_plane[2 + u : P : QUAD, :].bitcast(I32), d_plane[GROUP + u : P : QUAD, :].bitcast(I32))

        n3_t = load_list("n3_t", n3)
        n4_t = load_list("n4_t", n4)
        n5_t = load_list("n5_t", n5)

        d_picked = keep.tile([P, H], U32, name="d_picked")
        d_codes = keep.tile([P, H], U32, name="d_codes", align_bytes=64)
        nc.vector.tensor_copy(picked_bytes[:], x_scale_table[:].indirect(offs_t[:]))
        nc.vector.tensor_copy(d_picked[:], d_table[:].bitcast(U32).indirect(kidx_t[:]))
        nc.vector.tensor_copy(
            d_codes[:].rearrange("p (t m) -> p t m", t=PACK),
            d_picked[:].rearrange("p (m t) -> p t m", t=PACK),
        )
        x_codes = keep.tile([P, S], U32, name="x_codes", align_bytes=64)
        for a, b in HALVES:
            nc.vector.tensor_copy(x_codes[:, a:b], x_table[:].bitcast(U32).indirect(entries(offs_t, a, b)))

        w_raw = keep.tile([P, PACK, N], F32, name="w_raw", tag="x_then_w")
        nc.sync.dma_start(w_raw[:], w1.rearrange("(p j) c -> p j c", j=PACK))

        def product(dst, lhs_codes, lhs_plane, t, rhs_codes, rhs_plane):
            cols = slice(t * P, (t + 1) * P)
            nc.tensor.matmul_mx(
                out=dst,
                lhsT=lhs_codes[:, cols].bitcast(FP8X4),
                lhsT_scale=lhs_plane[:, cols],
                rhs=rhs_codes.bitcast(FP8X4),
                rhs_scale=rhs_plane,
                start=True,
                stop=True,
            )

        scaled = []
        gained = []
        banks = [psum.tile([P, S], F32, name=f"bank{t}") for t in range(PACK)]
        h_banks = [psum.tile([P, S], F32, name=f"h_bank{t}") for t in range(PACK)]
        for t in range(PACK):
            gained.append(keep.tile([P, S], F32, name=f"gained{t}"))
            scaled.append(keep.tile([P, S], F32, name=f"scaled{t}"))
            for a, b in HALVES if t == 0 else WHOLE:
                bank = banks[t] if a == 0 else h_banks[0]
                product(bank[:, a:b], d_codes, d_plane, t, x_codes[:, a:b], picked_bytes[:, a:b])
                nc.scalar.activation(gained[t][:, a:b], bank[:, a:b], ACT.Copy, scale=gain[:, t : t + 1])
                nc.scalar.activation(scaled[t][:, a:b], bank[:, a:b], ACT.Copy, scale=0.75 * 0.0625 * 0.0625)

        w_grouped = keep.tile([P, N * PACK], BF16, name="w_grouped", align_bytes=64)
        nc.scalar.copy(
            w_grouped[:].rearrange("p (t m j) -> p t m j", t=PACK, j=PACK),
            w_raw[:].rearrange("p j (m t) -> p t m j", t=PACK),
        )
        w_codes = keep.tile([P, N], U32, name="w_codes", align_bytes=64)
        w_plane = keep.tile([P, N], U8, name="w_plane", align_bytes=64)

        h_window = [keep.tile([P, 2 * S], F32, name=f"h_window{t}") for t in range(PACK)]
        h = [window[:, :S] for window in h_window]
        sq_here = [window[:, S:] for window in h_window]

        def terms(a, b, t, first, second, fetched, step):
            nc.vector.tensor_copy(fetched, gained[t][:].indirect(entries(n2_t, a, b)))
            nc.vector.tensor_tensor(first, scaled[t][:].indirect(entries(n1_t, a, b)), gained[t][:, a:b], MULT)
            for c in range(0, b - a, step):
                looked_up = scaled[t][:].indirect(entries(n3_t, a + c, a + c + step))
                nc.vector.tensor_tensor(second[:, c : c + step], looked_up, fetched[:, c : c + step], MULT)

        def quantised(a, b, z):
            z_codes = keep.tile([P, b - a], U32, name=f"z_codes{a}", align_bytes=64)
            z_plane = keep.tile([P, b - a], U8, name=f"z_plane{a}", align_bytes=64)
            nc.vector.quantize_mx(out=z_codes[:].bitcast(FP8X4), scales=z_plane[:], in_=z[:])
            return a, b, z_codes, z_plane

        def second_product(pieces):
            for t in range(PACK):
                for a, b, z_codes, z_plane in pieces:
                    product(h_banks[t][:, a:b], w_codes, w_plane, t, z_codes[:], z_plane[:])

        def square(dst, t, a, b):
            nc.scalar.activation(dst[t][:, a:b], h_banks[t][:, a:b], ACT.Square)

        firsts = [keep.tile([P, S], F32, name=f"first{t}") for t in range(PACK)]
        seconds = [keep.tile([P, S], F32, name=f"second{t}") for t in range(PACK)]
        fetcheds = [keep.tile([P, TURNED], F32, name=f"fetched{i}") for i in range(2)]
        blocks = range(TURNED // P)
        turned = [banks[j][:].rearrange("q (t p) -> q t p", t=PACK) for j in blocks]
        for t in range(PACK):
            first = firsts[t][:, :TURNED]
            second = seconds[t][:, :TURNED]
            terms(0, TURNED, t, first, second, fetcheds[t % 2][:], P if t == LAST else TURNED)
            for j in blocks:
                for term, opens in ((first, True), (second, False)):
                    block = term[:, j * P : (j + 1) * P]
                    nc.tensor.matmul(turned[j][:, t, :], block, ident[:], start=opens, stop=not opens, is_transpose=True)
        nc.vector.quantize_mx(out=w_codes[:].bitcast(FP8X4), scales=w_plane[:], in_=w_grouped[:])

        turned_z = []
        for (a, b), bank in zip(TURNED_PIECES, (banks[len(blocks)], banks[0])):
            z = keep.tile([P, (b - a) * PACK], BF16, name=f"z{a}", align_bytes=64)
            turned_z.append(z)
            back = bank[:, : 2 * (b - a)].rearrange("p (j u q) -> p j u q", u=2, q=P)
            for j in range(a // P, b // P):
                pairs = w_raw[:, j, : 2 * P]
                nc.scalar.copy(
                    pairs.bitcast(BF16).rearrange("q (u p e) -> q u p e", u=2, e=2),
                    turned[j].rearrange("q (u e) p -> q u p e", u=2),
                )
                for u in range(2):
                    nc.tensor.transpose(back[:, j - a // P, u, :], pairs[:, u * P : (u + 1) * P], ident[:])
            nc.scalar.copy(
                z[:].bitcast(F32).rearrange("p (j q u) -> p j q u", q=P, u=2),
                back.rearrange("p j u q -> p j q u"),
            )
        second_product([quantised(a, b, z) for (a, b), z in zip(TURNED_PIECES, turned_z)])

        for dst, t in ((sq, 0), (sq_here, 0), (sq, 1)):
            square(dst, t, 0, TURNED)

        first = firsts[LAST][:].rearrange("p (t j) -> p t j", t=PACK)
        second = seconds[LAST - 1][:].rearrange("p (t j) -> p t j", t=PACK)
        for t in range(PACK):
            fetched = turned_z[0][:].bitcast(F32) if t == LAST else fetcheds[t % 2]
            terms(TURNED, S, t, first[:, t, :], second[:, t, :], fetched[:, : S - TURNED], S - TURNED)
        z = keep.tile([P, (S - TURNED) * PACK], BF16, name=f"z{TURNED}", align_bytes=64)
        nc.vector.tensor_tensor(
            z[:].rearrange("p (g i t) -> p g t i", i=PACK, t=PACK),
            first.rearrange("p t (g i) -> p g t i", i=PACK),
            second.rearrange("p t (g i) -> p g t i", i=PACK),
            ADD,
        )
        second_product([quantised(TURNED, S, z)])

        out_rows = out.rearrange("(p t) j -> p t j", t=PACK)
        inv = [keep.tile([P, S], F32, name=f"inv{t}") for t in range(PACK)]

        def denominators(t):
            for a, b in HALVES if t == 0 else WHOLE:
                total = keep.tile([P, b - a], F32, name=f"total{t}_{a}")
                nc.vector.tensor_tensor(total[:], sq_window[t][:].indirect(entries(n4_t, a, b)), sq_here[t][:, a:b], ADD)
                nc.scalar.activation(inv[t][:, a:b], total[:], ACT.Abs_reciprocal_sqrt, bias=quarter[:])

        def results(t):
            for a, b in TAPER if t == LAST else WHOLE:
                res = keep.tile([P, b - a], F32, name=f"res{t}_{a}")
                nc.vector.tensor_tensor(res[:], h_window[t][:].indirect(entries(n5_t, a, b)), inv[t][:, a:b], MULT)
                nc.sync.dma_start(out_rows[:, t, a:b], res[:])

        for pair in ((0, 1), (2, 3)):
            for t in pair:
                square(sq, t, TURNED if t <= 1 else 0, S)
                square(sq_here, t, TURNED if t == 0 else 0, S)
            for t in pair:
                nc.scalar.copy(h[t], h_banks[t][:])
                denominators(t)
            for t in pair:
                results(t)
